import numpy as np, ml_dtypes
CORES = [2,3,42,43,82,83,122,123]
N = 8
import mx_ref
BF = ml_dtypes.bfloat16
def gentries(a):
    return np.ascontiguousarray(a.reshape(8, 16, -1).transpose(0, 2, 1)).reshape(8, -1)
def gtable(e):
    e = np.asarray(e); return np.ascontiguousarray(e.reshape(8, -1, 16).transpose(0, 2, 1)).reshape(128, -1).astype(np.int32)
def gcols(t, e):
    v = np.concatenate([t.reshape(8, 16, -1, 4), np.zeros((8, 16, 1, 4), BF)], axis=2)
    return np.ascontiguousarray(np.stack([v[g][:, e[g]] for g in range(8)])).reshape(128, -1)
def gpick(z, e):
    return np.concatenate([z[16 * g:16 * g + 16][:, e[g]] for g in range(8)])
def tile(rs):
    return np.stack(rs, axis=2).reshape(128, -1).astype(BF)
def pick(q, e):
    c = np.concatenate([q[0].reshape(128, -1, 4), np.zeros((128, 1, 4), np.uint8)], axis=1); s = np.concatenate([q[1], np.ones((16, 1), np.uint8)], axis=1)
    return (np.ascontiguousarray(c[:, e].reshape(128, -1)), np.ascontiguousarray(s[:, e]))
def join(*qs):
    return (np.concatenate([q[0] for q in qs], axis=1), np.concatenate([q[1] for q in qs], axis=1))
def put(q, e, v):
    c, s = q[0].reshape(128, -1, 4).copy(), q[1].copy(); c[:, e] = v[0].reshape(128, -1, 4); s[:, e] = v[1]
    return (c.reshape(128, -1), s)
def pk(c, s):
    return (np.ascontiguousarray(c), mx_ref.live(s))
def emit(q):
    return q[0], q[1]
def packed(v, rng):
    q = [mx_ref.quantize(np.ascontiguousarray(v[r])) for r in range(N)]
    return np.stack([a for a, b in q]), np.stack([mx_ref.plane(b, rng) for a, b in q])
def values_of_codes():
    e, c = np.zeros((128, 128, 4), np.float32), np.zeros((128, 2, 4), np.uint8)
    e[np.arange(128), np.arange(128), 0] = 1
    c[:127, :, 0] = np.arange(256).reshape(2, 128).T[:127]
    return mx_ref.matmul(mx_ref.quantize(e.reshape(128, 512).astype(BF)), (c.reshape(128, 8), np.full((16, 2), 127, np.uint8))).T.reshape(-1).astype(np.float64)
CODE_VALUE, SCALE_VALUE = values_of_codes(), 2.0 ** (np.arange(256) - 127.0)
def decode(q):
    return (CODE_VALUE[q[0]].reshape(16, 8, -1, 4) * SCALE_VALUE[q[1]][:, None, :, None] + 0.0).reshape(128, -1).astype(np.float32)
def f(rng, *shape):
    return mx_ref.flush((rng.standard_normal(shape, dtype=np.float32) * np.exp2(rng.integers(-2, 3, shape[:-1] + (1,)))).astype(BF))
def wide(rng, *shape, cols=0):
    v = rng.standard_normal(shape, dtype=np.float32) * np.exp2(rng.integers(-12, 13, shape)).astype(np.float32)
    if cols: v *= np.repeat(np.exp2(rng.integers(-cols, cols + 1, shape[:-2] + (1, shape[-1] // 4))) * (rng.random(shape[:-2] + (1, shape[-1] // 4)) > 0.0625), 4, axis=-1).astype(np.float32)
    return mx_ref.flush(v.astype(BF))
C, R = 320, 3
DECIDE = [0, 1, 2, 16, 32, 48, 64, 80, 96, 112]
def big(a):
    a = a.astype(np.float32)
    a[np.abs(a) < np.float32(2.0 ** -16)] = 0
    return a
def numbers_of(rng):
    return big(f(rng, N, 128, 4 * C)).reshape(N, 8, 16, C, 4), f(rng, N, 128, 512).astype(np.float32).reshape(N, 8, 16, 128, 4), f(rng, N, 128, 512).astype(np.float32).reshape(N, 8, 16, 128, 4)
def layers(rng, still=[]):
    w = np.clip(big(f(rng, N, 128, 2048)), -1, 1).reshape(N, 8, 16, 4, 8, 16, 4)
    w[:, :, still] = 0
    w[:, :, :, :, :, still] = 0
    return w
def inputs(rng, x, u, v, p, w):
    x, u, v, w = [np.ascontiguousarray(a).astype(np.float32).reshape(N, 128, -1).astype(BF) for a in (x, u, v, w)]
    c, s = packed(w, rng)
    return {"x": x, "u": u, "v": v, "p": np.stack([gtable(p[r]) for r in range(N)]), "wc": c, "ws": s}
def pointers(rng):
    return rng.integers(0, C, (N, 8, C))
def setup_inputs(rng):
    x, u, v = numbers_of(rng)
    return inputs(rng, x, u, v, pointers(rng), layers(rng))
def setup_inputs_ties(rng):
    x, u, v = numbers_of(rng)
    o = rng.permutation(N)
    k = rng.integers(0, 3, (N, 8, C, 4))
    k[:, :, :, 2] -= 1
    k[:, :, :, 3] = 0
    k[o[1], :, :, 2] = 1
    x[:, :, 0] = k
    h = np.ones(N)
    h[o[0]] = 0
    h[o[1]] = -1
    u[:, :, :, DECIDE] = 0
    for g in range(8): u[:, g, 0, 16 * g, 0] = h
    u[:, 0, 0, 1, 1] = 1
    u[:, 0, 0, 2, 2] = 1
    u[o[2], :, :, 1] = 0
    u[o[3], :, :, 2] = 0
    return inputs(rng, x, u, v, pointers(rng), layers(rng, [0]))
def setup_inputs_near(rng):
    x, u, v = numbers_of(rng)
    hold = [0, 1] + [i for i in range(8, 16)]
    x[:, :, hold] = 0
    u[:, :, :, DECIDE] = 0
    o = rng.permutation(N) % 4
    e = 2.0 ** -30
    for r in range(N):
        k = 1.0 if o[r] == 0 else e
        s, n = rng.integers(0, 16, (8, C)), rng.integers(0, 16, C)
        c, m = rng.integers(0, 2, C) * 2.0 - 1.0, rng.integers(0, 2, C) * 2.0 - 1.0
        z = rng.integers(-1, 2, C)
        x[r, :, 8] = ((s[:, :, None] >> np.arange(4)) & 1) * np.exp2(np.arange(4) - 23.0)
        x[r, 0, 9] = ((n[:, None] >> np.arange(4)) & 1) * np.exp2(np.arange(4) - 23.0)
        if o[r] < 2:
            x[r, :, 0, :, 0] = c
            x[r, :, 11, :, 0] = 2.0 ** -10
            x[r, 0, 1, :, 0] = m
            x[r, 0, 12, :, 0] = 2.0 ** -10
            x[r, 1, 9, :, 0] = z * 2.0 ** -23
            u[r, 0, 1, 1, 0] = k
            u[r, 0, 12, 1, 0] = k
            u[r, 1, 9, 2, 0] = k
        elif o[r] == 2:
            x[r, :, 0, :, 0] = np.where(c < 0, -1.0, 0.0)
            x[r, 0, 1, :, 0] = np.where(rng.permutation(C) % 8 == 0, m, 0.0)
            x[r, 1, 13, :, 0] = z * e
            u[r, 0, 1, 1, 0] = 1
            u[r, 1, 13, 2, 0] = e
        else:
            x[r, :, 10, :, 0] = rng.integers(1, 3, (8, C)) * c * np.where(np.arange(8) < 4, e, 1.125 * e)[:, None]
            x[r, 0, 14, :, 0] = rng.integers(-2, 3, C) * e
            x[r, 1, 13, :, 0] = z * 1.125 * e
            x[r, 1, 14, :, 0] = (0 - z) * 1.25 * e
            u[r, 0, 14, 1, 0] = e
            u[r, 1, 13, 2, 0] = 1.125 * e
            u[r, 1, 14, 2, 0] = e
        if o[r] < 3: u[r, 0, 9, 1] = k
        far = rng.permutation(8)
        for g in range(8):
            if o[r] < 2:
                u[r, g, 0, 16 * g, 0] = k
                u[r, g, 11, 16 * g, 0] = k
            if o[r] == 2 and g in far[:2]: u[r, g, 0, 16 * g, 0] = 1
            if o[r] < 3: u[r, g, 8, 16 * g] = k
            else: u[r, g, 10, 16 * g, 0] = 1.25 * e if g < 4 else 1.125 * e
    return inputs(rng, x, u, v, pointers(rng), layers(rng, hold))
def setup_inputs_late(rng):
    x, u, v = numbers_of(rng)
    x[:, :, 0] = (rng.permutation(N) % 2 * 0.0625)[:, None, None, None]
    u[:, :, :, DECIDE] = 0
    for g in range(8): u[:, g, 0, 16 * g, 0] = 1
    u[:, 0, 0, 1, 1] = 1
    u[:, 0, 0, 2, 2] = 1
    return inputs(rng, x, u, v, pointers(rng), layers(rng))
def setup_inputs_ends(rng):
    x, u, v = numbers_of(rng)
    o, h = rng.permutation(N), rng.permutation(8)
    p = pointers(rng)
    x[:] = np.where(rng.random((N, 8, 1, C, 1)) < 0.5, 0.875, 1.0) * 2.0 ** 25
    v[:] = (rng.integers(0, 2, (N, 1, 1, 128, 1)) * 2.0 - 1.0) * 2.0 ** 30
    u[:, :, :, DECIDE] = 2.0 ** 30
    for g in range(8): u[:, g, :, 16 * g] = 2.0 ** 29
    u[:, :, :, 2] = 0
    u[:, 0, :, 2] = 2.0 ** 30
    u[:, 1, :, 2] = -2.0 ** 30
    p[o[0]] = C - 1
    x[o[0], :, :, :C - 1] = 2.0 ** -30
    u[o[0], :, :, 2] = -2.0 ** 30
    p[o[1]] = 0
    x[o[1]] = 2.0 ** 25
    u[o[1], :, :, ::16] = 2.0 ** 30
    u[o[1], :, :, 2] = 2.0 ** 30
    p[o[2], h[:4]] = C - 1
    p[o[2], h[4:]] = 0
    p[o[2], 0] = rng.permutation(C)
    x[o[2], :, :, 1 + rng.permutation(C - 2)[:C // 2]] = 2.0 ** -30
    u[o[2], :, :, ::16] = -2.0 ** 30
    u[o[2], 0, :, 112] = -2.0 ** 29
    u[o[2], :, :, 1] *= -1
    u[o[2], :, :, 2] = 2.0 ** 30
    for g in h[:4]: u[o[3], :, :, 16 * g] *= -1
    u[o[3], :, :, 3:16] = 2.0 ** -30
    v[o[3]] = 2.0 ** -30
    return inputs(rng, x, u, v, p, np.ones((N, 128, 2048)))
def setup_inputs_spread(rng):
    x, u, v = numbers_of(rng)
    return inputs(rng, big(wide(rng, N, 128, 4 * C, cols=6)), u, v, pointers(rng), layers(rng))
def check_inputs(d):
    b = []
    for k, top in (("x", 2.0 ** 25), ("u", 2.0 ** 30), ("v", 2.0 ** 30)):
        a = np.abs(d[k].astype(np.float32))
        if not (np.isfinite(a).all() and ((a == 0) | (a >= 2.0 ** -30) & (a <= top)).all()): b.append("a value of " + k)
    if not ((d["p"] >= 0) & (d["p"] < C)).all(): b.append("an entry of p")
    none, least, most = [emit(mx_ref.quantize(np.full((128, 16), k, np.float32).astype(BF)))[1][0, 0] for k in (0.0, 2.0 ** -30, 1.0)]
    for r in range(N):
        if ((d["wc"][r] == 0x7F) | (d["wc"][r] == 0xFF)).any(): b.append("wc: a code that is no number")
        s = mx_ref.live(d["ws"][r])
        if ((s != none) & ((s < least) | (s > most))).any(): b.append("ws: a scale out of range")
        with np.errstate(all="ignore"):
            if not (np.abs(decode(pk(d["wc"][r], d["ws"][r]))) <= 1).all(): b.append("a number of W beyond 1 in size")
    return b
def reference(x, u, v, p, wc, ws):
    qu = [mx_ref.quantize(u[r]) for r in range(N)]
    lay = [pk(wc[r], ws[r]) for r in range(N)]
    first = np.stack([gentries(p[r]) for r in range(N)])
    ptr = first.copy()
    now = [x[r] for r in range(N)]
    g, j = np.arange(8)[:, None], np.arange(C)
    for t in range(R):
        sent, via = [], []
        for r in range(N):
            s = mx_ref.matmul(qu[r], mx_ref.quantize(now[r])) + np.float32(0.0)
            level = np.argmax(s[::16], axis=0)
            o = np.argsort(-s[1], kind="stable")
            c = np.zeros(C, np.int64)
            c[o] = np.roll(o, -1)
            call = s[2] > 0
            new = np.where((g < level) & call, ptr[r][:, c], ptr[r])
            new = np.where(g == level, np.where(call, j, first[r]), new)
            ptr[r] = new
            via.append(new[:, c])
            sent.append(mx_ref.quantize(gcols(now[r], new)))
        for r in range(N):
            q = sent[(r - 1 - t) % N]
            h = [mx_ref.matmul(pick(lay[r], np.arange(128 * b, 128 * b + 128)), q) * np.float32(0.00390625) for b in range(4)]
            now[r] = tile([gpick(h[b], via[r]) + now[r][:, b::4].astype(np.float32) for b in range(4)])
    y, op = np.zeros((N, 128, C), np.float32), np.zeros((N, 8, C), np.float32)
    oc, osc = np.zeros((N, 128, 4 * C), np.uint8), np.zeros((N, 16, C), np.uint8)
    for r in range(N):
        q = mx_ref.quantize(now[r])
        y[r] = mx_ref.matmul(mx_ref.quantize(v[r]), q)
        op[r] = ptr[r]
        oc[r], osc[r] = emit(q)
    return {"y": y, "op": op, "oc": oc, "osc": osc}

from concourse.mybir import dt, AluOpType as A, ActivationFunctionType as F

C, R = 320, 3
HALF = [(0, 160), (160, 320)]
PIECE = [0, 128, 192]
NUM, FIRST, PTR, WIN = 328, 648, 968, 1288
STEP = 262144.0
ORDER = 1

SCRATCH = {"ps": ("psum", [128, 4096], "float32")}
for _d, _names in (
        ("bfloat16", "xa 1280 xb 1280 z 1280 ut 512 vt 512 edge 128 ones 128 df 384 cmp 960 junk 960"),
        ("float8_e4m3fn_x4", "qu 128 qo 128 qv 128 qw 512 qx 320 qz0 320 qz1 320 qz2 320 land0 320 land1 320 land2 320"),
        ("uint8", "su 128 so 128 sv 128 sw 512 sx 320 sz0 320 sz1 320 sz2 320 sland0 320 sland1 320 sland2 320"),
        ("int32", "prow 320 dzi 320 pi 1 pm 1 gi 1 kdi 20 mi 20 tm 8 m2 20 tr 8 rank 20"),
        ("uint16", "m16 20 one16 8 rk16 20 rp16 20 off16 20 via16 20 d16_0 20 d16_1 20 d16_2 20 d16_3 20"),
        ("float32", "win0 1288 win1 1288 nwin 328 pf 320 dz 320 kc 16 kdn 20 kcl 20 zero8 8 pr 6 pmx 24 lev 3 c8 3 m2s 3 mx1 1 mk 32 "
                    "mt 32 mb 128 sm 128 lt 20 b1 20 b2 20 b3 20 b4 20 b5 20 base 20 junk2 24 cn 2 rk 64 rt 64 rb 192 sr 192 o1 20 o2 20 "
                    "sc 320 scv 320 vrow 320 yb 320 h0 320 h1 320 h2 320 h3 320")):
    _w = _names.split()
    for _i in range(0, len(_w), 2):
        SCRATCH[_w[_i]] = ("sbuf", [128, int(_w[_i + 1])], _d)

LOADS = {"ld_u": 1, "ld_x": 2, "ld_p": 16, "ld_w": 2, "ld_v": 1, "st_op": 1, "st_c": 5, "st_y": 1}
SEMAPHORES = ["c_v", "c_s", "c_t", "c_g", "sent"] + list(LOADS) + ["arr%d_%d" % (t, h) for t in range(R) for h in range(len(HALF))]


def tracker(g, T):
    queues = {"g": g, "v": g.vector, "s": g.scalar, "t": g.tensor, "y": g.sync}
    hist, known, count, snaps = {}, {q: {} for q in queues}, {q: 0 for q in queues}, {}

    def clash(a, b):
        return a[1] < b[2] and b[1] < a[2] and not (a[3] > 1 and a[3] == b[3] and a[1] % a[3] != b[1] % b[3])

    def need(q, sem, val):
        if known[q].get(sem, 0) < val:
            queues[q].wait_ge(T.sem[sem], val)
            known[q][sem] = val
            for k, w in snaps.get((sem, val), {}).items():
                known[q][k] = max(known[q].get(k, 0), w)

    def note(regs, write, q, sem, val):
        for r in regs:
            hist.setdefault(r[0], []).append((r, write, q, sem, val))

    def issue(q, call, reads, writes, sem=None, val=None):
        wants = {}
        for regs, write in ((reads, False), (writes, True)):
            for r in regs:
                for (b, w, q2, s2, v2) in hist.get(r[0], []):
                    if clash(r, b) and (w or write or r[0] == "ps" and q2 != q):
                        wants[s2] = max(wants.get(s2, 0), v2)
        if q == "g" and count[q]:
            wants["c_g"] = count[q]
        for s2, v2 in sorted(wants.items(), key=lambda i: -len(snaps.get(i, {}))):
            need(q, s2, v2)
        inst = call(queues[q])
        if sem is not None:
            inst.then_inc(T.sem[sem], 16)
        else:
            count[q] += 1
            sem, val = "c_" + q, count[q]
            inst.then_inc(T.sem[sem], 1)
            snaps[(sem, val)] = dict(known[q])
        note(reads, False, q, sem, val)
        note(writes, True, q, sem, val)

    return issue, need, note, count


def rank_program(g, core, T, topo):
    rank = T.rank_of(core)
    if rank is None:
        return
    N = len(T.cores)
    issue, need, note, count = tracker(g, T)

    def ap(r):
        return T[r[0]][:, r[1]:r[2]:r[3]] if r[3] > 1 else T[r[0]][:, r[1]:r[2]]

    def V(name, a=None, b=None, step=1):
        return (name, 0, SCRATCH[name][1][1], 1) if a is None else (name, a, b, step)

    def bank(k, a=0, b=C, step=1):
        return ("ps", 512 * k + a, 512 * k + b, step)

    def regs(*rs):
        rs = [r for r in rs if r is not None and not isinstance(r, (int, float))]
        return [("ps", r[1] // 512 * 512, r[1] // 512 * 512 + 512, 1) if r[0] == "ps" else r for r in rs]

    def arg(s):
        return s if s is None or isinstance(s, (int, float)) else ap(s)

    def picked(src, off):
        return ap(src) if off is None else ap(src).indirect(ap(off))

    def copy(out, src, off=None):
        issue("v", lambda e: e.tensor_copy(ap(out), picked(src, off)), regs(src, off), regs(out))

    def scopy(out, src, off=None, scale=1.0):
        issue("s", lambda e: e.activation(ap(out), picked(src, off), F.Copy, scale=scale), regs(src, off), regs(out))

    def scatter(win, off, src):
        issue("v", lambda e: e.tensor_copy(ap(win).indirect(ap(off)), ap(src)), regs(src, off), regs(win))

    def ts(out, src, s1, op0, s2=None, *op1):
        issue("v", lambda e: e.tensor_scalar(ap(out), ap(src), arg(s1), arg(s2), op0, *op1), regs(src, s1, s2), regs(out))

    def tt(out, a, b, op, off=None):
        issue("v", lambda e: e.tensor_tensor(ap(out), picked(a, off), ap(b), op), regs(a, b, off), regs(out))

    def scan(out, d0, d1, initial):
        issue("v", lambda e: e.tensor_tensor_scan(ap(out), ap(d0), ap(d1), initial, A.add, A.max), regs(d0, d1), regs(out))

    def turn(out, src):
        issue("v", lambda e: e.transpose(ap(out), ap(src)), regs(src), regs(out))

    def act(out, src, func, bias=0.0, scale=1.0, accum=None):
        issue("s", lambda e: e.activation(ap(out), ap(src), func, bias=arg(bias), scale=scale, accum_out=arg(accum)),
              regs(src, bias), regs(out, accum))

    def fill(out, c):
        issue("v", lambda e: e.memset(ap(out), c), [], regs(out))

    def iota(out, pattern, base, cm, **k):
        issue("g", lambda e: e.iota(ap(out), pattern, base, cm, **k), [], regs(out))

    def quant(q, s, src):
        issue("v", lambda e: e.quantize_mx(ap(q), ap(s), ap(src)), regs(src), regs(q, s))

    def mm(out, q1, s1, q2, s2):
        issue("t", lambda e: e.matmul_mx(ap(out), ap(q1), ap(s1), ap(q2), ap(s2), True, True), regs(q1, s1, q2, s2), regs(out))

    def dma(q, sem, out, src, reads, writes):
        issue(q, lambda e: e.dma_start(out, src), reads, writes, sem, 16 * LOADS[sem])

    def bcast(out, name, part, a, b):
        issue("g", lambda e: e.partition_broadcast(ap(out), T[name][part:part + 1, a:b], 128), regs((name, a, b, 1)), regs(out))

    dma("y", "ld_u", T.ut[:], T.u[:], [], [V("ut")])
    dma("s", "ld_x", T.xa[:, 0:640], T.x[:, 0:640], [], [V("xa", 0, 640)])
    dma("y", "ld_x", T.xa[:, 640:1280], T.x[:, 640:1280], [], [V("xa", 640, 1280)])
    for i in range(16):
        dma("sy"[i % 2], "ld_p", T.prow[i:128:16, :], T.p[:], [], [V("prow")] if i == 15 else [])
    dma("y", "ld_w", T.qw[:].bitcast(dt.uint8), T.wc[:], [], [V("qw")])
    dma("y", "ld_w", T.sw[:], T.ws[:], [], [V("sw")])
    dma("y", "ld_v", T.vt[:], T.v[:], [], [V("vt")])

    fill(V("one16"), ORDER)
    fill(V("ones"), 1e-30)
    fill(V("zero8"), 0.0)
    fill(V("mk"), 0.0)
    fill(V("rk"), 0.0)
    for w in ("win0", "win1"):
        fill(V(w, C, NUM), 0.0)
    iota(V("pi"), [[1, 1]], 0, 1)
    iota(V("dzi"), [[0, 20], [-1, 16]], 128, 1)
    iota(V("mi"), [[1, 20]], 0, 0)
    iota(V("kdi"), [[16, 20]], PTR, 0)
    issue("g", lambda e: e.affine_select(T.edge[:], T.ones[:], [[-1, 128]], A.is_gt, -1e-30, 0, 1), regs(V("ones")), regs(V("edge")))
    for w in ("win0", "win1"):
        iota(V(w, NUM, FIRST), [[1, C]], 0, 0, allow_small_or_imprecise_dtypes=True)
    ts(V("pm"), V("pi"), 15, A.bitwise_and)
    ts(V("gi"), V("pi"), 4, A.arith_shift_right)
    PMF, P20, GB, GA, CST = [V("kc", i, i + 1) for i in range(5)]
    CT = [V("kc", 8 + i, 9 + i) for i in range(4)]
    copy(PMF, V("pm"))
    ts(P20, V("pm"), 20.0, A.mult)
    copy(GB, V("gi"))
    ts(GA, V("gi"), 8.0, A.add)
    ts(CST, V("pm"), -STEP, A.mult, 15 * STEP, A.add)
    for k in range(4):
        ts(CT[k], V("pm"), 4 * STEP, A.mult, k - 60 * STEP, A.add)
    ts(V("m16"), V("mi"), P20, A.add)
    ts(V("kdn"), V("kdi"), PMF, A.add)
    ts(V("kcl"), V("kdn"), -1.0, A.mult, 1.0, A.add)
    ts(V("dzi"), V("dzi"), 15, A.bitwise_and)
    ts(V("dz"), V("dzi"), 0.0, A.is_equal, -65 * STEP, A.mult)
    ts(V("dz"), V("dz"), STEP, A.add)

    quant(V("qu"), V("su"), V("ut"))
    issue("v", lambda e: e.tensor_copy(T.qo[:].bitcast(dt.uint32), T.qu[:].bitcast(dt.uint32).indirect(T.one16[:])), regs(V("qu"), V("one16")), regs(V("qo")))
    issue("s", lambda e: e.activation(T.so[:], T.su[:].indirect(T.one16[:]), F.Copy), regs(V("su"), V("one16")), regs(V("so")))

    quant(V("qx"), V("sx"), V("xa"))
    for t in range(R):
        cur, new = "win%d" % (t % 2), "win%d" % (1 - t % 2)
        xo, xn = ("xa", "xb") if t % 2 == 0 else ("xb", "xa")
        mm(bank(0), V("qo"), V("so"), V("qx"), V("sx"))
        for a in range(3):
            c = PIECE[a]
            mm(bank(1 + a, 0, 128), V("qx", c, c + 128), V("sx", c, c + 128), V("qu"), V("su"))
        mm(bank(4), V("qo"), V("so"), V("qx"), V("sx"))
        own = [V("pr", 2 * a, 2 * a + 1) for a in range(3)]
        for a in range(3):
            act(V("pr", 2 * a, 2 * a + 2), bank(1 + a, 1, 3), F.Copy)
        for a in range(3):
            scan(V("pmx", 8 * a, 8 * a + 8), V("zero8"), bank(1 + a, 0, 128, 16), -1e29)
            if a == 0:
                ts(V("cmp", 128, 320), bank(0, 128, 320), own[0], A.is_gt)
        for a in range(3):
            act(V("junk2", 8 * a, 8 * a + 8), V("pmx", 8 * a, 8 * a + 8), F.Sign, V("pmx", 8 * a + 7, 8 * a + 8), -1.0, V("lev", a, a + 1))
        ts(V("cmp", C, C + 128), bank(0, 0, 128), own[1], A.is_ge)
        ts(V("cmp", C + 256, C + 320), bank(0, 256, 320), own[1], A.is_gt)
        for a in range(3):
            act(V("df", 128 * a, 128 * a + 128), bank(4, PIECE[a], PIECE[a] + 128), F.Identity, own[a], -1.0)
        ts(V("c8"), V("pr", 1, 6, 2), 0.0, A.is_gt, 8.0, A.mult)
        tt(V("m2s"), V("c8"), V("lev"), A.add)
        ts(V("mx1"), V("m2s", 1, 2), 16.0, A.mult, V("m2s", 0, 1), A.add)
        ts(V("mk", 0, 1), V("m2s", 2, 3), 256.0, A.mult, V("mx1"), A.add)
        turn(V("mt"), V("mk"))
        for k in range(4):
            bcast(V("mb", 32 * k, 32 * k + 32), "mt", 32 * k, 0, 32)
        ts(V("cmp", 2 * C, 2 * C + 192), bank(0, 0, 192), own[2], A.is_ge)
        for a in range(3):
            c = C * a + PIECE[a]
            tt(V("cmp", c, c + 128), V("df", 128 * a, 128 * a + 128), V("edge"), A.is_lt)
            act(V("junk", C * a, C * a + C), V("cmp", C * a, C * a + C), F.Copy, accum=V("cn", a, a + 1) if a < 2 else V("rk", 32, 33))
        ts(V("rk", 0, 1), V("cn", 1, 2), 512.0, A.mult, V("cn", 0, 1), A.add)
        turn(V("rt"), V("rk"))
        for k, lo in enumerate((0, 32, 64, 128)):
            w = 32 if k < 2 else 64
            bcast(V("rb", lo, lo + w), "rt", 32 * k, 0, w)
        if t == 0:
            copy(V("pf"), V("prow"))
            copy(V("win0", PTR, WIN), V("pf"), V("m16"))
            for w in ("win0", "win1"):
                scopy(V(w, FIRST, PTR), V("win0", PTR, WIN))
        scan(V("sm"), V("dz", 0, 128), V("mb"), 0.0)
        ts(V("tm"), V("sm", 15, 128, 16), CST, A.subtract)
        ts(V("m2", 0, 8), V("tm"), 15, A.bitwise_and)
        ts(V("m2", 8, 16), V("tm"), 4, A.arith_shift_right, 15, A.bitwise_and)
        ts(V("m2", 16, 20), V("tm", 4, 8), 8, A.arith_shift_right)
        ts(V("lt"), V("m2"), GA, A.is_gt)
        ts(V("b1"), V("m2"), GA, A.is_equal, float(NUM - PTR), A.mult)
        ts(V("b2"), V("m2"), GB, A.is_equal, float(FIRST - PTR), A.mult)
        tt(V("b3"), V("lt"), V("kcl"), A.mult)
        tt(V("b4"), V("b1"), V("b2"), A.add)
        tt(V("b5"), V("b3"), V("kdn"), A.add)
        tt(V("base"), V("b4"), V("b5"), A.add)
        scan(V("sr"), V("dz", 0, 192), V("rb"), 0.0)
        ts(V("tr", 0, 6), V("sr", 15, 96, 16), CST, A.subtract)
        ts(V("tr", 6, 8), V("sr", 143, 160, 16), CST, A.subtract)
        ts(V("rank", 16, 18), V("sr", 111, 128, 16), CST, A.subtract)
        ts(V("rank", 18, 20), V("sr", 175, 192, 16), CST, A.subtract)
        ts(V("rank", 0, 8), V("tr"), 511, A.bitwise_and)
        ts(V("rank", 8, 16), V("tr"), 9, A.arith_shift_right)
        copy(V("rk16"), V("rank"))
        scatter(V(cur, 0, C), V("rk16"), V(cur, PTR, WIN))
        scopy(V(cur, C, C + 1), V(cur, 0, 1))
        tt(V("o1"), V("rank"), V("lt"), A.mult)
        tt(V("o2"), V("o1"), V("base"), A.add)
        copy(V("off16"), V("o2"))
        copy(V(new, PTR, WIN), V(cur), V("off16"))
        if t == R - 1:
            dma("y", "st_op", T.op[:], T[new][0:128:16, PTR:WIN], [V(new, PTR, WIN)], [])
        scan(V("sc"), V("dz"), V(new, PTR, WIN), 0.0)
        for k in (0, 2, 1, 3):
            ts(V("d16_%d" % k), V("sc", 15, C, 16), 4.0, A.mult, CT[k], A.add)
        dst = T.cores[(rank + 1 + t) % N]
        rid, pid, _ = topo.addr(dst)
        mask = sum(1 << e for e in topo.engines(core, dst)[:8])
        qz, sz, ld, sl = "qz%d" % t, "sz%d" % t, "land%d" % t, "sland%d" % t
        for h, (a, b) in enumerate(HALF):
            for k in range(4):
                (scopy if k < 2 else copy)(V("z", 4 * a + k, 4 * b, 4), V(xo), V("d16_%d" % k, a // 16, b // 16))
            quant(V(qz, a, b), V(sz, a, b), V("z", 4 * a, 4 * b))
            need("g", "c_v", count["v"])
            arr = T.sem["arr%d_%d" % (t, h)]
            g.remote_dma(T[ld][:, a:b].bitcast(dt.uint8), T[qz][:, a:b].bitcast(dt.uint8), arr, T.sem.sent, pid, rid, mask)
            g.remote_dma(T[sl][:, a:b], T[sz][:, a:b], arr, T.sem.sent, pid, rid, mask)
            note([V(ld, a, b), V(sl, a, b)], True, "far", "arr%d_%d" % (t, h), 16)
        scatter(V("nwin", 0, C), V("rk16"), V(new, PTR, WIN))
        scopy(V("nwin", C, C + 1), V("nwin", 0, 1))
        ts(V("rp16"), V("rank"), 1.0, A.add)
        scopy(V("vrow"), V("nwin", 0, C + 1), V("rp16"))
        scan(V("scv"), V("dz"), V("vrow"), 0.0)
        ts(V("via16"), V("scv", 15, C, 16), CST, A.subtract)
        if t == 0:
            quant(V("qv"), V("sv"), V("vt"))
        for h, (a, b) in enumerate(HALF):
            for k in range(4):
                o = bank(2 * k + h, 0, b - a)
                mm(o, V("qw", 128 * k, 128 * k + 128), V("sw", 128 * k, 128 * k + 128), V(ld, a, b), V(sl, a, b))
                scopy(V("h%d" % k, a, b), o, scale=0.00390625)
        for k in range(4):
            tt(V(xn, k, 4 * C, 4), V("h%d" % k), V(xo, k, 4 * C, 4), A.add, off=V("via16"))
        quant(V("qx"), V("sx"), V(xn))

    mm(bank(0), V("qv"), V("sv"), V("qx"), V("sx"))
    dma("y", "st_c", T.oc[:], T.qx[:].bitcast(dt.uint8), [V("qx")], [])
    for i in range(4):
        dma("ys"[i % 2], "st_c", T.osc[4 * i:4 * i + 4, :], T.sx[32 * i:32 * i + 4, :], [V("sx")], [])
    copy(V("yb"), bank(0))
    dma("y", "st_y", T.y[:], T.yb[:], [V("yb")], [])
    for s in ("st_op", "st_c", "st_y"):
        need("y", s, 16 * LOADS[s])
    need("g", "sent", 4 * R * 8)
    for q in "vstg":
        need("g", "c_" + q, count[q])
